import numpy as np
import ml_dtypes


def mxq(x, axis, fmt="e4m3"):
    dtype, down = {"e4m3": (ml_dtypes.float8_e4m3fn, 7), "e5m2": (ml_dtypes.float8_e5m2, 14)}[fmt]
    v = np.moveaxis(np.asarray(x, np.float32).astype(ml_dtypes.bfloat16).astype(np.float64), axis, -1)
    blocks = v.reshape(v.shape[:-1] + (-1, 32))
    amax = np.abs(blocks).max(-1, keepdims=True)
    byte = np.maximum(np.where(amax > 0, np.frexp(amax)[1] - 1 + 127, 0) - down, 1)
    scale = np.exp2(byte - 127.0)
    codes = (blocks / scale).astype(np.float32).astype(dtype).astype(np.float64)
    return np.moveaxis((codes * scale).reshape(v.shape), -1, axis)


WIDE = False


def mx_kscale(k):
    if not WIDE:
        return np.ones(k)
    levels = np.array([10, -10, 5, -5, 0])
    if k % 512:
        return np.exp2(np.random.permutation(np.resize(levels, k // 32))).repeat(32)
    a = np.empty((k // 512, 16))
    for p in range(k // 512):
        a[p, :8] = np.random.permutation(np.resize(levels, 8))
        for g in range(8):
            far = levels[np.abs(levels - a[p, g]) >= 10]
            a[p, g + 8] = far[np.random.randint(len(far))]
    return np.exp2(a.ravel()).repeat(32)


def f64(x):
    return np.asarray(x).astype(np.float64)


def striped(idx):
    return np.tile(idx.reshape(-1, 16).T, (8, 1)).astype(np.uint16)


def unstriped(offs):
    return offs[:16].T.reshape(-1).astype(np.int64)


def striped8(idx):
    return np.concatenate([x.reshape(-1, 16).T for x in idx]).astype(np.uint16)


def runs(offs, k):
    lists = np.stack([offs[16 * r : 16 * r + 16].T.reshape(-1) for r in range(8)]).astype(np.int64)
    return lists[np.arange(k) % 512 // 64]


def pack_weight(w):
    k, n = w.shape
    w = f64(np.asarray(w, np.float32).astype(ml_dtypes.bfloat16)).reshape(k // 32, 32, n)
    amax = np.abs(w).max(1)
    byte = np.clip(np.where(amax > 0, np.frexp(amax)[1] - 1 + 127 - 7, 1), 1, 254)
    scaled = (w * np.exp2(127.0 - byte)[:, None, :]).reshape(k, n).astype(np.float32)
    words = np.ascontiguousarray(scaled.reshape(k // 512, 128, 4, n).transpose(0, 1, 3, 2)).astype(ml_dtypes.float8_e4m3fn).view(np.uint8)
    return words, np.ascontiguousarray(byte.astype(np.uint8).reshape(k // 512, 16, n))


def unpack_weight(words, scales):
    g, p, n, _ = words.shape
    vals = np.ascontiguousarray(words).view(ml_dtypes.float8_e4m3fn).astype(np.float64) * np.repeat(np.exp2(scales.astype(np.float64) - 127.0), 8, axis=1)[..., None]
    return vals.transpose(0, 1, 3, 2).reshape(g * 512, n)


K, T, S, N, H = 512, 2048, 512, 512, 512


def setup_inputs():
    n = np.random.standard_normal
    s = mx_kscale(K)[:, None]
    u = mx_kscale(H)
    packed_xT = pack_weight(n((K, T)) * s)
    return {
        "x_words": packed_xT[0],
        "x_scales": packed_xT[1],
        "w1": (n((K, H)) / np.sqrt(K) / s).astype(np.float32),
        "gn": (np.random.uniform(0.5, 1.5, (H, 1)) * u[:, None]).astype(np.float32),
        "w2": (n((H, H)) / np.sqrt(H) / u[:, None]).astype(np.float32),
        "res": n((N, S)).astype(np.float32),
        "w3": (n((H, N)) / np.sqrt(H) / u[:, None]).astype(np.float32),
        "offs": striped(np.random.permutation(T)[:S]),
        "n1": striped8(np.stack([np.random.permutation(S) for _ in range(8)])),
        "n2": striped8(np.stack([np.random.permutation(S) for _ in range(8)])),
        "mv": striped8(np.stack([np.random.permutation(S) for _ in range(8)])),
    }


def reference(x_words, x_scales, w1, gn, w2, res, w3, offs, n1, n2, mv):
    xq = unpack_weight(x_words, x_scales)[:, unstriped(offs)]
    y = mxq(f64(w1), 0, "e4m3").T @ xq
    a = y - (y[np.arange(H)[:, None], runs(n1, H)])
    b = y - (y[np.arange(H)[:, None], runs(n2, H)])
    z = f64(gn) * (np.log(np.exp(a) + np.exp(-1.0 * a)) - (np.log(np.exp(b) + np.exp(-1.0 * b))))
    h = np.tanh(mxq(f64(w2), 0, "e4m3").T @ mxq(z, 0, "e4m3"))
    z2 = f64(gn) * (h[np.arange(H)[:, None], runs(mv, H)])
    return f64(res) + (mxq(f64(w3), 0, "e4m3").T @ mxq(z2, 0, "e4m3"))

@@ -1,0 +1,269 @@
+from contextlib import ExitStack
+
+import concourse.mybir as mybir
+from concourse.masks import make_identity
+
+K, T, S, H, N = 512, 2048, 512, 512, 512
+FLOPS = 2 * S * (K * H + H * H + H * N)
+
+F32 = mybir.dt.float32
+BF16 = mybir.dt.bfloat16
+I32 = mybir.dt.int32
+U32 = mybir.dt.uint32
+U16 = mybir.dt.uint16
+U8 = mybir.dt.uint8
+FP8X4 = mybir.dt.float8_e4m3fn_x4
+ALU = mybir.AluOpType
+ACT = mybir.ActivationFunctionType
+
+P = 128
+PACK = 4
+CHUNKS = S // P
+HALF = S // 2
+LAST_CHUNKS = ((0, 256), (256, 384), (384, 512))
+
+
+def tile_picked_logcosh2_none_p_kernel(
+    tc, x_words, x_scales, w1, gn, w2, res, w3, offs, n1, n2, mv, out
+):
+    nc = tc.nc
+    with ExitStack() as ctx:
+        keep = ctx.enter_context(tc.tile_pool(name="keep", bufs=1))
+        psum = ctx.enter_context(tc.psum_pool(name="psum", bufs=1))
+
+        def bank(index, name):
+            return psum.tile([P, S], F32, tag="bank%d" % index, name=name)
+
+        def load_list(source, name):
+            offsets = keep.tile([P, S // 16], U16, name=name)
+            nc.sync.dma_start(offsets[:], source)
+            return offsets
+
+        def load_weight(weight, name, pieces):
+            width = H // pieces
+            tiles = []
+            for piece in range(pieces):
+                raw = keep.tile([P, PACK, width], F32, name="%s_raw%d" % (name, piece))
+                rows = weight.rearrange("(p j) c -> p j c", j=PACK)
+                nc.sync.dma_start(raw[:], rows[:, :, piece * width : (piece + 1) * width])
+                tiles.append(raw)
+            return tiles
+
+        def bf16_tile(columns, name, tag=None):
+            return keep.tile([P, columns * PACK], BF16, align_bytes=64, name=name, tag=tag or name)
+
+        def mx_tiles(name):
+            codes = keep.tile([P, S], U32, align_bytes=64, name=name + "_codes")
+            scales = keep.tile([P, S], U8, align_bytes=64, name=name + "_scales")
+            return codes, scales
+
+        def quantize(operand, lo, hi, grouped):
+            codes, scales = operand
+            nc.vector.quantize_mx(out=codes[:, lo:hi].bitcast(FP8X4), scales=scales[:, lo:hi], in_=grouped)
+
+        def product(target, weight, t, moving_codes, moving_scales):
+            nc.tensor.matmul_mx(
+                out=target,
+                lhsT=weight[0][:, t * P : (t + 1) * P].bitcast(FP8X4),
+                lhsT_scale=weight[1][:, t * P : (t + 1) * P],
+                rhs=moving_codes.bitcast(FP8X4),
+                rhs_scale=moving_scales,
+                start=True,
+                stop=True,
+            )
+
+        def deal_columns(copy, grouped, raw, m_lo, m_hi, first):
+            dealt = grouped[:].rearrange("p (t m j) -> p m j t", t=PACK, j=PACK)
+            source = raw[:].rearrange("p j (m t) -> p m j t", t=PACK)
+            copy(dealt[:, m_lo:m_hi], source[:, m_lo - first : m_hi - first])
+
+        def add_turned(target, source, start, stop):
+            nc.tensor.matmul(target, source, identity[:], start=start, stop=stop, is_transpose=True)
+
+        offs_sb = load_list(offs, "offs_sb")
+        words = keep.tile([P, T], U32, name="words")
+        nc.sync.dma_start(words[:].bitcast(I32), x_words[0].rearrange("p n t -> p (n t)").bitcast(I32))
+        bytes_all = keep.tile([P, T], U8, name="bytes_all")
+        nc.vector.memset(bytes_all[:].bitcast(I32), 0)
+        for q in range(4):
+            nc.scalar.dma_start(
+                bytes_all[32 * q : 32 * q + 4, :].bitcast(I32), x_scales[0][4 * q : 4 * q + 4, :].bitcast(I32)
+            )
+        w1_raw = load_weight(w1, "w1", 2)
+        n1_sb = load_list(n1, "n1_sb")
+        n2_sb = load_list(n2, "n2_sb")
+        gain = keep.tile([P, PACK], F32, name="gain")
+        nc.sync.dma_start(gain[:], gn.rearrange("(p t) o -> p (t o)", t=PACK))
+        w2_raw = load_weight(w2, "w2", 1)
+        mv_sb = load_list(mv, "mv_sb")
+        w3_raw = load_weight(w3, "w3", 1)
+        res_sb = keep.tile([P, PACK, S], F32, name="res_sb")
+        nc.sync.dma_start(res_sb[:], res.rearrange("(t p) j -> p t j", p=P))
+
+        identity = keep.tile([P, P], F32, name="identity")
+        make_identity(nc, identity[:])
+        last_gain = keep.tile([P, 2], F32, name="last_gain")
+        nc.gpsimd.tensor_scalar(last_gain[:, 0:1], gain[:, 3:4], 2.0, 0.0, ALU.mult, ALU.add)
+        nc.gpsimd.tensor_scalar(last_gain[:, 1:2], gain[:, 3:4], -1.0, 0.0, ALU.mult, ALU.add)
+
+        x_scale = keep.tile([P, S], U8, align_bytes=64, name="x_scale")
+        x_codes = keep.tile([P, S], U32, align_bytes=64, name="x_codes")
+        nc.vector.tensor_copy(x_scale[:], bytes_all[:].indirect(offs_sb[:]))
+        nc.vector.tensor_copy(x_codes[:], words[:].indirect(offs_sb[:]))
+
+        w1_mx = mx_tiles("w1")
+        w1_bf16 = bf16_tile(H, "w1_bf16")
+        deal_columns(nc.scalar.copy, w1_bf16, w1_raw[0], 0, 64, 0)
+        deal_columns(nc.scalar.copy, w1_bf16, w1_raw[1], 64, 88, 64)
+        deal_columns(nc.vector.tensor_copy, w1_bf16, w1_raw[1], 88, 128, 64)
+        y = []
+        for t in range(PACK):
+            quantize(w1_mx, t * P, (t + 1) * P, w1_bf16[:, t * S : (t + 1) * S])
+        for t in range(PACK):
+            sums = bank(t, "y_sums%d" % t)
+            product(sums[:], w1_mx, t, x_codes[:], x_scale[:])
+            y_t = keep.tile([P, S], F32, align_bytes=64, name="y%d" % t)
+            nc.scalar.copy(y_t[:], sums[:])
+            y.append(y_t)
+
+        z_sums = [bank(c, "z_sums%d" % c) for c in range(CHUNKS)]
+        tails = keep.tile([P, CHUNKS, 2, PACK, P], F32, align_bytes=64, name="tails")
+        all_sizes = []
+        for t in range(PACK):
+            sizes = keep.tile([P, 2, S], F32, align_bytes=64, name="sizes%d" % t)
+            others = keep.tile([P, 2, S], F32, name="others%d" % t)
+            all_sizes.append(sizes)
+            for side, places in enumerate((n1_sb, n2_sb)):
+                other = others[:, side, :]
+                for lo in (0, HALF):
+                    nc.vector.tensor_scalar(
+                        other[:, lo : lo + HALF],
+                        y[t][:].indirect(places[:, lo // 16 : (lo + HALF) // 16]),
+                        -1.0,
+                        0.0,
+                        ALU.mult,
+                        ALU.add,
+                    )
+                diff = bank(4 + 2 * (t % 2) + side, "diff%d_%d" % (t, side))
+                for c in range(CHUNKS):
+                    cols = slice(c * P, (c + 1) * P)
+                    add_turned(diff[:, cols], y[t][:, cols], c == 0, False)
+                for c in range(CHUNKS):
+                    cols = slice(c * P, (c + 1) * P)
+                    add_turned(diff[:, cols], other[:, cols], False, c == CHUNKS - 1)
+                nc.scalar.activation(sizes[:, side, :], diff[:], ACT.Abs)
+            for lo, hi in ((0, 2),) if t + 1 < PACK else ((0, 1), (1, 2)):
+                nc.scalar.activation(
+                    tails[:, :, lo:hi, t, :].rearrange("p c s f -> p s c f"),
+                    sizes[:, lo:hi, :].rearrange("p s (c f) -> p s c f", f=P),
+                    ACT.Tanh,
+                )
+
+        w2_mx = mx_tiles("w2")
+        w2_bf16 = bf16_tile(H, "w2_bf16", "y3")
+        deal_columns(nc.vector.tensor_copy, w2_bf16, w2_raw[0], 0, 128, 0)
+        linear = keep.tile([P, PACK, S], F32, name="linear", tag="others3")
+        for t in range(PACK):
+            nc.vector.tensor_tensor(linear[:, t, :], all_sizes[t][:, 0, :], all_sizes[t][:, 1, :], ALU.subtract)
+            for c in range(CHUNKS):
+                add_turned(z_sums[c][:, t * P : (t + 1) * P], linear[:, t, c * P : (c + 1) * P], t == 0, False)
+        quantize(w2_mx, 0, H, w2_bf16[:])
+
+        z_mx = mx_tiles("z")
+        h_sums = [bank(4 + t, "h_sums%d" % t) for t in range(PACK)]
+        gain_by_place = gain[:].unsqueeze(1).to_broadcast([P, P, PACK])
+        def curved_part(c):
+            logs = keep.tile([P, 2, PACK, P], F32, align_bytes=64, name="logs%d" % c)
+            nc.scalar.activation(
+                logs[:].rearrange("p s t f -> p (s t f)"),
+                tails[:, c].rearrange("p s t f -> p (s t f)"),
+                ACT.Ln,
+                bias=1.0,
+            )
+            if c == CHUNKS - 1:
+                warm = keep.tile([P, 1], F32, name="warm")
+                nc.scalar.activation(warm[:], logs[:, 0, 0, 0:1], ACT.Sigmoid)
+            curved = keep.tile([P, PACK, P], F32, name="curved%d" % c)
+            nc.vector.tensor_tensor(curved[:], logs[:, 1], logs[:, 0], ALU.subtract)
+            for t in range(PACK):
+                add_turned(z_sums[c][:, t * P : (t + 1) * P], curved[:, t, :], False, t == PACK - 1)
+
+        def finish_z(c):
+            z_bf16 = bf16_tile(P, "z_bf16_%d" % c, "logs%d" % (c + 1) if c + 1 < CHUNKS else None)
+            nc.vector.tensor_tensor(
+                z_bf16[:].rearrange("p (j t) -> p j t", t=PACK),
+                z_sums[c][:].rearrange("p (t j) -> p j t", t=PACK),
+                gain_by_place,
+                ALU.mult,
+            )
+            quantize(z_mx, c * P, (c + 1) * P, z_bf16[:])
+            for lo, hi in LAST_CHUNKS:
+                if hi == (c + 1) * P:
+                    for t in range(PACK):
+                        product(h_sums[t][:, lo:hi], w2_mx, t, z_mx[0][:, lo:hi], z_mx[1][:, lo:hi])
+
+        curved_part(0)
+        for c in range(CHUNKS):
+            if c + 1 < CHUNKS:
+                curved_part(c + 1)
+            finish_z(c)
+
+        w3_mx = mx_tiles("w3")
+        w3_bf16 = bf16_tile(N, "w3_bf16", "tails")
+        nc.scalar.copy(
+            w3_bf16[:].rearrange("p (c i j) -> p c j i", i=PACK, j=PACK),
+            w3_raw[0][:].rearrange("p j (c i) -> p c j i", i=PACK),
+        )
+        quantize(w3_mx, 0, N, w3_bf16[:])
+
+        gained = []
+        last_sums = keep.tile([P, S], F32, name="last_sums")
+        nc.vector.tensor_copy(last_sums[:], h_sums[PACK - 1][:])
+        for t in range(PACK - 1):
+            h_t = keep.tile([P, S], F32, name="h%d" % t)
+            nc.scalar.activation(h_t[:], h_sums[t][:], ACT.Tanh)
+            gained_t = keep.tile([P, S], F32, name="gained%d" % t)
+            if t < 2:
+                nc.vector.tensor_scalar(gained_t[:], h_t[:], gain[:, t : t + 1], None, ALU.mult)
+            else:
+                nc.scalar.activation(gained_t[:], h_t[:], ACT.Copy, scale=gain[:, t : t + 1])
+            gained.append(gained_t)
+
+        z2_mx = mx_tiles("z2")
+        out_rows = out.rearrange("(t p) j -> p t j", p=P)
+        next_bank = 0
+        moved_first = keep.tile([P, PACK, HALF], BF16, name="moved_first")
+        moved_later = keep.tile([P, 2, PACK, P], BF16, name="moved_later", tag="h2")
+        for lo, hi in LAST_CHUNKS:
+            width = hi - lo
+            moved = moved_first if lo == 0 else moved_later[:, (lo - HALF) // P]
+            places = mv_sb[:, lo // 16 : hi // 16]
+            for t in range(PACK - 1):
+                nc.vector.tensor_copy(moved[:, t, :], gained[t][:].indirect(places))
+            logistic = keep.tile([P, width], F32, name="logistic%d" % lo)
+            nc.scalar.activation(logistic[:], last_sums[:].indirect(places), ACT.Sigmoid, scale=2.0)
+            nc.scalar.activation(
+                moved[:, PACK - 1, :], logistic[:], ACT.Identity, scale=last_gain[:, 0:1], bias=last_gain[:, 1:2]
+            )
+            z2_bf16 = bf16_tile(width, "z2_bf16_%d" % lo)
+            nc.scalar.copy(
+                z2_bf16[:].rearrange("p (c i t) -> p c t i", i=PACK, t=PACK),
+                moved[:, :, :].rearrange("p t (c i) -> p c t i", i=PACK),
+            )
+            quantize(z2_mx, lo, hi, z2_bf16[:])
+            per_bank = S // width
+            for t0 in range(0, PACK, per_bank):
+                sums = bank(next_bank, "out_sums%d" % next_bank)
+                next_bank = next_bank + 1
+                for t in range(t0, t0 + per_bank):
+                    product(
+                        sums[:, (t - t0) * width : (t - t0 + 1) * width], w3_mx, t, z2_mx[0][:, lo:hi], z2_mx[1][:, lo:hi]
+                    )
+                result = keep.tile([P, per_bank, width], F32, name="result%d" % next_bank)
+                nc.vector.tensor_tensor(
+                    result[:],
+                    sums[:].rearrange("p (t j) -> p t j", j=width),
+                    res_sb[:, t0 : t0 + per_bank, lo:hi],
+                    ALU.add,
+                )
+                nc.sync.dma_start(out_rows[:, t0 : t0 + per_bank, lo:hi], result[:])

@@ -40,20 +40,18 @@ def tile_picked_logcosh2_none_p_kernel(
             return offsets
 
         def load_weight(weight, name, pieces):
-            width = H // pieces
             tiles = []
-            for piece in range(pieces):
-                raw = keep.tile([P, PACK, width], F32, name="%s_raw%d" % (name, piece))
-                rows = weight.rearrange("(p j) c -> p j c", j=PACK)
-                nc.sync.dma_start(raw[:], rows[:, :, piece * width : (piece + 1) * width])
+            for lo, hi in pieces:
+                raw = keep.tile([P, PACK, hi - lo], F32, name="%s_raw%d" % (name, lo))
+                nc.sync.dma_start(raw[:], weight.rearrange("(p j) c -> p j c", j=PACK)[:, :, lo:hi])
                 tiles.append(raw)
             return tiles
 
         def bf16_tile(columns, name, tag=None):
             return keep.tile([P, columns * PACK], BF16, align_bytes=64, name=name, tag=tag or name)
 
-        def mx_tiles(name):
-            codes = keep.tile([P, S], U32, align_bytes=64, name=name + "_codes")
+        def mx_tiles(name, tag=None):
+            codes = keep.tile([P, S], U32, align_bytes=64, name=name + "_codes", tag=tag or name + "_codes")
             scales = keep.tile([P, S], U8, align_bytes=64, name=name + "_scales")
             return codes, scales
 
@@ -84,19 +82,19 @@ def tile_picked_logcosh2_none_p_kernel(
         words = keep.tile([P, T], U32, name="words")
         nc.sync.dma_start(words[:].bitcast(I32), x_words[0].rearrange("p n t -> p (n t)").bitcast(I32))
         bytes_all = keep.tile([P, T], U8, name="bytes_all")
-        nc.vector.memset(bytes_all[:].bitcast(I32), 0)
+        nc.gpsimd.memset(bytes_all[:].bitcast(I32), 0)
         for q in range(4):
             nc.scalar.dma_start(
                 bytes_all[32 * q : 32 * q + 4, :].bitcast(I32), x_scales[0][4 * q : 4 * q + 4, :].bitcast(I32)
             )
-        w1_raw = load_weight(w1, "w1", 2)
+        w1_raw = load_weight(w1, "w1", ((0, 256), (256, 512)))
         n1_sb = load_list(n1, "n1_sb")
         n2_sb = load_list(n2, "n2_sb")
+        w2_raw = load_weight(w2, "w2", ((0, H),))
         gain = keep.tile([P, PACK], F32, name="gain")
         nc.sync.dma_start(gain[:], gn.rearrange("(p t) o -> p (t o)", t=PACK))
-        w2_raw = load_weight(w2, "w2", 1)
         mv_sb = load_list(mv, "mv_sb")
-        w3_raw = load_weight(w3, "w3", 1)
+        w3_raw = load_weight(w3, "w3", ((0, N),))
         res_sb = keep.tile([P, PACK, S], F32, name="res_sb")
         nc.sync.dma_start(res_sb[:], res.rearrange("(t p) j -> p t j", p=P))
 
@@ -106,6 +104,11 @@ def tile_picked_logcosh2_none_p_kernel(
         nc.gpsimd.tensor_scalar(last_gain[:, 0:1], gain[:, 3:4], 2.0, 0.0, ALU.mult, ALU.add)
         nc.gpsimd.tensor_scalar(last_gain[:, 1:2], gain[:, 3:4], -1.0, 0.0, ALU.mult, ALU.add)
 
+        gain_first = keep.tile([P, PACK - 1, HALF], F32, align_bytes=64, name="gain_first")
+        nc.gpsimd.tensor_copy(gain_first[:], gain[:, 0 : PACK - 1].unsqueeze(2).to_broadcast([P, PACK - 1, HALF]))
+        gain_later = keep.tile([P, PACK - 1, P], F32, name="gain_later")
+        nc.gpsimd.tensor_copy(gain_later[:], gain[:, 0 : PACK - 1].unsqueeze(2).to_broadcast([P, PACK - 1, P]))
+
         x_scale = keep.tile([P, S], U8, align_bytes=64, name="x_scale")
         x_codes = keep.tile([P, S], U32, align_bytes=64, name="x_codes")
         nc.vector.tensor_copy(x_scale[:], bytes_all[:].indirect(offs_sb[:]))
@@ -114,51 +117,64 @@ def tile_picked_logcosh2_none_p_kernel(
         w1_mx = mx_tiles("w1")
         w1_bf16 = bf16_tile(H, "w1_bf16")
         deal_columns(nc.scalar.copy, w1_bf16, w1_raw[0], 0, 64, 0)
-        deal_columns(nc.scalar.copy, w1_bf16, w1_raw[1], 64, 88, 64)
-        deal_columns(nc.vector.tensor_copy, w1_bf16, w1_raw[1], 88, 128, 64)
+        deal_columns(nc.scalar.copy, w1_bf16, w1_raw[1], 64, 84, 64)
+        deal_columns(nc.vector.tensor_copy, w1_bf16, w1_raw[1], 84, 128, 64)
         y = []
         for t in range(PACK):
             quantize(w1_mx, t * P, (t + 1) * P, w1_bf16[:, t * S : (t + 1) * S])
         for t in range(PACK):
+            y_t = keep.tile([P, 2 * S], F32, align_bytes=64, name="y%d" % t)
             sums = bank(t, "y_sums%d" % t)
-            product(sums[:], w1_mx, t, x_codes[:], x_scale[:])
-            y_t = keep.tile([P, S], F32, align_bytes=64, name="y%d" % t)
-            nc.scalar.copy(y_t[:], sums[:])
+            if t == 0:
+                second = bank(7, "y_sums0_second")
+                product(sums[:, :HALF], w1_mx, t, x_codes[:, :HALF], x_scale[:, :HALF])
+                product(second[:, :HALF], w1_mx, t, x_codes[:, HALF:], x_scale[:, HALF:])
+                nc.scalar.copy(y_t[:, :HALF], sums[:, :HALF])
+                nc.vector.tensor_copy(y_t[:, HALF:S], second[:, :HALF])
+            else:
+                product(sums[:], w1_mx, t, x_codes[:], x_scale[:])
+                nc.scalar.copy(y_t[:, :S], sums[:])
             y.append(y_t)
 
-        z_sums = [bank(c, "z_sums%d" % c) for c in range(CHUNKS)]
         tails = keep.tile([P, CHUNKS, 2, PACK, P], F32, align_bytes=64, name="tails")
         all_sizes = []
+        diff_banks = [4, 5, 6, 7, 0, 1, 2, 3, 4]
+        waiting = []
+
+        def squash():
+            t, side, lo, hi = waiting.pop(0)
+            nc.scalar.activation(
+                tails[:, lo // P : hi // P, side, t, :],
+                all_sizes[t][:, side, lo:hi].rearrange("p (c f) -> p c f", f=P),
+                ACT.Tanh,
+            )
+
         for t in range(PACK):
             sizes = keep.tile([P, 2, S], F32, align_bytes=64, name="sizes%d" % t)
             others = keep.tile([P, 2, S], F32, name="others%d" % t)
             all_sizes.append(sizes)
             for side, places in enumerate((n1_sb, n2_sb)):
-                other = others[:, side, :]
-                for lo in (0, HALF):
+                for lo, hi in ((0, HALF), (HALF, S)) if t == PACK - 1 and side == 1 else ((0, S),):
+                    other = others[:, side, lo:hi]
                     nc.vector.tensor_scalar(
-                        other[:, lo : lo + HALF],
-                        y[t][:].indirect(places[:, lo // 16 : (lo + HALF) // 16]),
-                        -1.0,
-                        0.0,
-                        ALU.mult,
-                        ALU.add,
+                        other, y[t][:].indirect(places[:, lo // 16 : hi // 16]), -1.0, 0.0, ALU.mult, ALU.add
                     )
-                diff = bank(4 + 2 * (t % 2) + side, "diff%d_%d" % (t, side))
-                for c in range(CHUNKS):
-                    cols = slice(c * P, (c + 1) * P)
-                    add_turned(diff[:, cols], y[t][:, cols], c == 0, False)
-                for c in range(CHUNKS):
-                    cols = slice(c * P, (c + 1) * P)
-                    add_turned(diff[:, cols], other[:, cols], False, c == CHUNKS - 1)
-                nc.scalar.activation(sizes[:, side, :], diff[:], ACT.Abs)
-            for lo, hi in ((0, 2),) if t + 1 < PACK else ((0, 1), (1, 2)):
-                nc.scalar.activation(
-                    tails[:, :, lo:hi, t, :].rearrange("p c s f -> p s c f"),
-                    sizes[:, lo:hi, :].rearrange("p s (c f) -> p s c f", f=P),
-                    ACT.Tanh,
-                )
+                    diff = bank(diff_banks.pop(0), "diff%d_%d_%d" % (t, side, lo))
+                    for at in range(0, hi - lo, P):
+                        add_turned(diff[:, at : at + P], y[t][:, lo + at : lo + at + P], at == 0, False)
+                    for at in range(0, hi - lo, P):
+                        add_turned(diff[:, at : at + P], other[:, at : at + P], False, at + P == hi - lo)
+                    nc.scalar.activation(sizes[:, side, lo:hi], diff[:, : hi - lo], ACT.Abs)
+                    if waiting:
+                        squash()
+                    waiting.append((t, side, lo, hi))
+        squash()
 
+        one = keep.tile([P, 1], F32, name="one")
+        nc.scalar.activation(one[:], all_sizes[PACK - 1][:, 1, S - 1 : S], ACT.Identity, scale=0.0, bias=1.0)
+        z_banks = (0, 1, 5, 6)
+        h_banks = (2, 3, 4, 7)
+        z_sums = [bank(z_banks[c], "z_sums%d" % c) for c in range(CHUNKS)]
         w2_mx = mx_tiles("w2")
         w2_bf16 = bf16_tile(H, "w2_bf16", "y3")
         deal_columns(nc.vector.tensor_copy, w2_bf16, w2_raw[0], 0, 128, 0)
@@ -169,44 +185,45 @@ def tile_picked_logcosh2_none_p_kernel(
                 add_turned(z_sums[c][:, t * P : (t + 1) * P], linear[:, t, c * P : (c + 1) * P], t == 0, False)
         quantize(w2_mx, 0, H, w2_bf16[:])
 
-        z_mx = mx_tiles("z")
-        h_sums = [bank(4 + t, "h_sums%d" % t) for t in range(PACK)]
+        h_sums = [bank(h_banks[t], "h_sums%d" % t) for t in range(PACK)]
         gain_by_place = gain[:].unsqueeze(1).to_broadcast([P, P, PACK])
         def curved_part(c):
             logs = keep.tile([P, 2, PACK, P], F32, align_bytes=64, name="logs%d" % c)
-            nc.scalar.activation(
-                logs[:].rearrange("p s t f -> p (s t f)"),
-                tails[:, c].rearrange("p s t f -> p (s t f)"),
-                ACT.Ln,
-                bias=1.0,
-            )
+            curved = keep.tile([P, PACK, P], F32, align_bytes=64, name="curved%d" % c)
+            for lo, hi in ((0, 2), (2, PACK)) if c == CHUNKS - 1 else ((0, PACK),):
+                nc.scalar.activation(logs[:, :, lo:hi, :], tails[:, c, :, lo:hi, :], ACT.Ln, bias=one[:])
+                nc.vector.tensor_scalar(curved[:, lo:hi], logs[:, 0, lo:hi], -1.0, None, ALU.mult)
+                for t in range(lo, hi):
+                    add_turned(z_sums[c][:, t * P : (t + 1) * P], logs[:, 1, t, :], False, False)
+                for t in range(lo, hi):
+                    add_turned(z_sums[c][:, t * P : (t + 1) * P], curved[:, t, :], False, t == PACK - 1)
             if c == CHUNKS - 1:
                 warm = keep.tile([P, 1], F32, name="warm")
-                nc.scalar.activation(warm[:], logs[:, 0, 0, 0:1], ACT.Sigmoid)
-            curved = keep.tile([P, PACK, P], F32, name="curved%d" % c)
-            nc.vector.tensor_tensor(curved[:], logs[:, 1], logs[:, 0], ALU.subtract)
-            for t in range(PACK):
-                add_turned(z_sums[c][:, t * P : (t + 1) * P], curved[:, t, :], False, t == PACK - 1)
+                nc.scalar.activation(warm[:], logs[:, 0, PACK - 1, 0:1], ACT.Sigmoid)
 
-        def finish_z(c):
-            z_bf16 = bf16_tile(P, "z_bf16_%d" % c, "logs%d" % (c + 1) if c + 1 < CHUNKS else None)
+        z_bf16 = bf16_tile(S, "z_bf16")
+
+        def finish_z(c, z_mx):
             nc.vector.tensor_tensor(
-                z_bf16[:].rearrange("p (j t) -> p j t", t=PACK),
+                z_bf16[:, c * S : (c + 1) * S].rearrange("p (j t) -> p j t", t=PACK),
                 z_sums[c][:].rearrange("p (t j) -> p j t", t=PACK),
                 gain_by_place,
                 ALU.mult,
             )
-            quantize(z_mx, c * P, (c + 1) * P, z_bf16[:])
-            for lo, hi in LAST_CHUNKS:
-                if hi == (c + 1) * P:
+            for lo, hi in ((0, HALF), (HALF, S)):
+                if c == CHUNKS - 1 - (lo == 0):
+                    quantize(z_mx, lo, hi, z_bf16[:, PACK * lo : PACK * hi])
                     for t in range(PACK):
                         product(h_sums[t][:, lo:hi], w2_mx, t, z_mx[0][:, lo:hi], z_mx[1][:, lo:hi])
 
         curved_part(0)
+        z_mx = None
         for c in range(CHUNKS):
             if c + 1 < CHUNKS:
                 curved_part(c + 1)
-            finish_z(c)
+            if c == CHUNKS - 2:
+                z_mx = mx_tiles("z", "curved3")
+            finish_z(c, z_mx)
 
         w3_mx = mx_tiles("w3")
         w3_bf16 = bf16_tile(N, "w3_bf16", "tails")
@@ -216,30 +233,26 @@ def tile_picked_logcosh2_none_p_kernel(
         )
         quantize(w3_mx, 0, N, w3_bf16[:])
 
-        gained = []
         last_sums = keep.tile([P, S], F32, name="last_sums")
         nc.vector.tensor_copy(last_sums[:], h_sums[PACK - 1][:])
+        h = []
         for t in range(PACK - 1):
             h_t = keep.tile([P, S], F32, name="h%d" % t)
             nc.scalar.activation(h_t[:], h_sums[t][:], ACT.Tanh)
-            gained_t = keep.tile([P, S], F32, name="gained%d" % t)
-            if t < 2:
-                nc.vector.tensor_scalar(gained_t[:], h_t[:], gain[:, t : t + 1], None, ALU.mult)
-            else:
-                nc.scalar.activation(gained_t[:], h_t[:], ACT.Copy, scale=gain[:, t : t + 1])
-            gained.append(gained_t)
+            h.append(h_t)
 
         z2_mx = mx_tiles("z2")
         out_rows = out.rearrange("(t p) j -> p t j", p=P)
-        next_bank = 0
-        moved_first = keep.tile([P, PACK, HALF], BF16, name="moved_first")
-        moved_later = keep.tile([P, 2, PACK, P], BF16, name="moved_later", tag="h2")
+        free_banks = list(z_banks)
+        finished = []
         for lo, hi in LAST_CHUNKS:
             width = hi - lo
-            moved = moved_first if lo == 0 else moved_later[:, (lo - HALF) // P]
+            behind = {0: "moved0", HALF: "gain_first", S - P: "z2_bf16_0"}[lo]
+            moved = keep.tile([P, PACK, width], F32, align_bytes=64, name="moved%d" % lo, tag=behind)
+            gain_wide = gain_first if lo == 0 else gain_later
             places = mv_sb[:, lo // 16 : hi // 16]
             for t in range(PACK - 1):
-                nc.vector.tensor_copy(moved[:, t, :], gained[t][:].indirect(places))
+                nc.vector.tensor_tensor(moved[:, t, :], h[t][:].indirect(places), gain_wide[:, t, :], ALU.mult)
             logistic = keep.tile([P, width], F32, name="logistic%d" % lo)
             nc.scalar.activation(logistic[:], last_sums[:].indirect(places), ACT.Sigmoid, scale=2.0)
             nc.scalar.activation(
@@ -253,17 +266,22 @@ def tile_picked_logcosh2_none_p_kernel(
             quantize(z2_mx, lo, hi, z2_bf16[:])
             per_bank = S // width
             for t0 in range(0, PACK, per_bank):
-                sums = bank(next_bank, "out_sums%d" % next_bank)
-                next_bank = next_bank + 1
+                sums = bank(free_banks.pop(0), "out_sums%d_%d" % (lo, t0))
                 for t in range(t0, t0 + per_bank):
                     product(
                         sums[:, (t - t0) * width : (t - t0 + 1) * width], w3_mx, t, z2_mx[0][:, lo:hi], z2_mx[1][:, lo:hi]
                     )
-                result = keep.tile([P, per_bank, width], F32, name="result%d" % next_bank)
+                finished.append((sums, lo, hi, t0))
+
+        for sums, lo, hi, t0 in finished:
+            width = hi - lo
+            step = 2 if hi == S else S // width
+            for t1 in range(t0, t0 + S // width, step):
+                result = keep.tile([P, step, width], F32, name="result%d_%d" % (lo, t1))
                 nc.vector.tensor_tensor(
                     result[:],
-                    sums[:].rearrange("p (t j) -> p t j", j=width),
-                    res_sb[:, t0 : t0 + per_bank, lo:hi],
+                    sums[:, (t1 - t0) * width : (t1 - t0 + step) * width].rearrange("p (t j) -> p t j", j=width),
+                    res_sb[:, t1 : t1 + step, lo:hi],
                     ALU.add,
                 )
-                nc.sync.dma_start(out_rows[:, t0 : t0 + per_bank, lo:hi], result[:])
+                nc.sync.dma_start(out_rows[:, t1 : t1 + step, lo:hi], result[:])

@@ -42,7 +42,7 @@ def tile_picked_logcosh2_none_p_kernel(
         def load_weight(weight, name, pieces):
             tiles = []
             for lo, hi in pieces:
-                raw = keep.tile([P, PACK, hi - lo], F32, name="%s_raw%d" % (name, lo))
+                raw = keep.tile([P, PACK, hi - lo], F32, align_bytes=64, name="%s_raw%d" % (name, lo))
                 nc.sync.dma_start(raw[:], weight.rearrange("(p j) c -> p j c", j=PACK)[:, :, lo:hi])
                 tiles.append(raw)
             return tiles
@@ -87,12 +87,12 @@ def tile_picked_logcosh2_none_p_kernel(
             nc.scalar.dma_start(
                 bytes_all[32 * q : 32 * q + 4, :].bitcast(I32), x_scales[0][4 * q : 4 * q + 4, :].bitcast(I32)
             )
-        w1_raw = load_weight(w1, "w1", ((0, 256), (256, 512)))
+        w1_raw = load_weight(w1, "w1", ((0, HALF), (HALF, H)))
+        gain = keep.tile([P, PACK], F32, name="gain")
+        nc.sync.dma_start(gain[:], gn.rearrange("(p t) o -> p (t o)", t=PACK))
         n1_sb = load_list(n1, "n1_sb")
         n2_sb = load_list(n2, "n2_sb")
         w2_raw = load_weight(w2, "w2", ((0, H),))
-        gain = keep.tile([P, PACK], F32, name="gain")
-        nc.sync.dma_start(gain[:], gn.rearrange("(p t) o -> p (t o)", t=PACK))
         mv_sb = load_list(mv, "mv_sb")
         w3_raw = load_weight(w3, "w3", ((0, N),))
         res_sb = keep.tile([P, PACK, S], F32, name="res_sb")
@@ -104,14 +104,10 @@ def tile_picked_logcosh2_none_p_kernel(
         nc.gpsimd.tensor_scalar(last_gain[:, 0:1], gain[:, 3:4], 2.0, 0.0, ALU.mult, ALU.add)
         nc.gpsimd.tensor_scalar(last_gain[:, 1:2], gain[:, 3:4], -1.0, 0.0, ALU.mult, ALU.add)
 
-        gain_first = keep.tile([P, PACK - 1, HALF], F32, align_bytes=64, name="gain_first")
-        nc.gpsimd.tensor_copy(gain_first[:], gain[:, 0 : PACK - 1].unsqueeze(2).to_broadcast([P, PACK - 1, HALF]))
-        gain_later = keep.tile([P, PACK - 1, P], F32, name="gain_later")
-        nc.gpsimd.tensor_copy(gain_later[:], gain[:, 0 : PACK - 1].unsqueeze(2).to_broadcast([P, PACK - 1, P]))
-
         x_scale = keep.tile([P, S], U8, align_bytes=64, name="x_scale")
         x_codes = keep.tile([P, S], U32, align_bytes=64, name="x_codes")
         nc.vector.tensor_copy(x_scale[:], bytes_all[:].indirect(offs_sb[:]))
+
         nc.vector.tensor_copy(x_codes[:], words[:].indirect(offs_sb[:]))
 
         w1_mx = mx_tiles("w1")
@@ -119,9 +115,13 @@ def tile_picked_logcosh2_none_p_kernel(
         deal_columns(nc.scalar.copy, w1_bf16, w1_raw[0], 0, 64, 0)
         deal_columns(nc.scalar.copy, w1_bf16, w1_raw[1], 64, 84, 64)
         deal_columns(nc.vector.tensor_copy, w1_bf16, w1_raw[1], 84, 128, 64)
-        y = []
         for t in range(PACK):
             quantize(w1_mx, t * P, (t + 1) * P, w1_bf16[:, t * S : (t + 1) * S])
+        gain_first = keep.tile([P, PACK - 1, HALF], F32, align_bytes=64, name="gain_first", tag="w1_raw256")
+        nc.scalar.copy(gain_first[:], gain[:, 0 : PACK - 1].unsqueeze(2).to_broadcast([P, PACK - 1, HALF]))
+        gain_later = keep.tile([P, PACK - 1, P], F32, name="gain_later")
+        nc.scalar.copy(gain_later[:], gain_first[:, :, :P])
+        y = []
         for t in range(PACK):
             y_t = keep.tile([P, 2 * S], F32, align_bytes=64, name="y%d" % t)
             sums = bank(t, "y_sums%d" % t)
@@ -149,25 +149,34 @@ def tile_picked_logcosh2_none_p_kernel(
                 ACT.Tanh,
             )
 
+        pieces = [(t, side, 0, S) for t in range(PACK) for side in range(2)][:-1]
+        pieces.extend([(PACK - 1, 1, 0, HALF), (PACK - 1, 1, HALF, S)])
+        all_others = []
         for t in range(PACK):
-            sizes = keep.tile([P, 2, S], F32, align_bytes=64, name="sizes%d" % t)
-            others = keep.tile([P, 2, S], F32, name="others%d" % t)
-            all_sizes.append(sizes)
-            for side, places in enumerate((n1_sb, n2_sb)):
-                for lo, hi in ((0, HALF), (HALF, S)) if t == PACK - 1 and side == 1 else ((0, S),):
-                    other = others[:, side, lo:hi]
-                    nc.vector.tensor_scalar(
-                        other, y[t][:].indirect(places[:, lo // 16 : hi // 16]), -1.0, 0.0, ALU.mult, ALU.add
-                    )
-                    diff = bank(diff_banks.pop(0), "diff%d_%d_%d" % (t, side, lo))
-                    for at in range(0, hi - lo, P):
-                        add_turned(diff[:, at : at + P], y[t][:, lo + at : lo + at + P], at == 0, False)
-                    for at in range(0, hi - lo, P):
-                        add_turned(diff[:, at : at + P], other[:, at : at + P], False, at + P == hi - lo)
-                    nc.scalar.activation(sizes[:, side, lo:hi], diff[:, : hi - lo], ACT.Abs)
-                    if waiting:
-                        squash()
-                    waiting.append((t, side, lo, hi))
+            all_sizes.append(keep.tile([P, 2, S], F32, align_bytes=64, name="sizes%d" % t))
+            all_others.append(keep.tile([P, 2, S], F32, name="others%d" % t))
+
+        def turn_own(index):
+            t, side, lo, hi = pieces[index]
+            diff = bank(diff_banks[index], "diff%d" % index)
+            for at in range(0, hi - lo, P):
+                add_turned(diff[:, at : at + P], y[t][:, lo + at : lo + at + P], at == 0, False)
+            return diff
+
+        next_diff = turn_own(0)
+        for index, (t, side, lo, hi) in enumerate(pieces):
+            diff = next_diff
+            if index + 1 < len(pieces):
+                next_diff = turn_own(index + 1)
+            other = all_others[t][:, side, lo:hi]
+            places = (n1_sb, n2_sb)[side][:, lo // 16 : hi // 16]
+            nc.vector.tensor_scalar(other, y[t][:].indirect(places), -1.0, 0.0, ALU.mult, ALU.add)
+            for at in range(0, hi - lo, P):
+                add_turned(diff[:, at : at + P], other[:, at : at + P], False, at + P == hi - lo)
+            nc.scalar.activation(all_sizes[t][:, side, lo:hi], diff[:, : hi - lo], ACT.Abs)
+            if waiting:
+                squash()
+            waiting.append((t, side, lo, hi))
         squash()
 
         one = keep.tile([P, 1], F32, name="one")
@@ -192,9 +201,12 @@ def tile_picked_logcosh2_none_p_kernel(
             curved = keep.tile([P, PACK, P], F32, align_bytes=64, name="curved%d" % c)
             for lo, hi in ((0, 2), (2, PACK)) if c == CHUNKS - 1 else ((0, PACK),):
                 nc.scalar.activation(logs[:, :, lo:hi, :], tails[:, c, :, lo:hi, :], ACT.Ln, bias=one[:])
-                nc.vector.tensor_scalar(curved[:, lo:hi], logs[:, 0, lo:hi], -1.0, None, ALU.mult)
-                for t in range(lo, hi):
-                    add_turned(z_sums[c][:, t * P : (t + 1) * P], logs[:, 1, t, :], False, False)
+                if c == CHUNKS - 1:
+                    nc.vector.tensor_tensor(curved[:, lo:hi], logs[:, 1, lo:hi], logs[:, 0, lo:hi], ALU.subtract)
+                else:
+                    nc.vector.tensor_scalar(curved[:, lo:hi], logs[:, 0, lo:hi], -1.0, None, ALU.mult)
+                    for t in range(lo, hi):
+                        add_turned(z_sums[c][:, t * P : (t + 1) * P], logs[:, 1, t, :], False, False)
                 for t in range(lo, hi):
                     add_turned(z_sums[c][:, t * P : (t + 1) * P], curved[:, t, :], False, t == PACK - 1)
             if c == CHUNKS - 1:
@@ -247,7 +259,7 @@ def tile_picked_logcosh2_none_p_kernel(
         finished = []
         for lo, hi in LAST_CHUNKS:
             width = hi - lo
-            behind = {0: "moved0", HALF: "gain_first", S - P: "z2_bf16_0"}[lo]
+            behind = {0: "moved0", HALF: "w1_raw256", S - P: "z2_bf16_0"}[lo]
             moved = keep.tile([P, PACK, width], F32, align_bytes=64, name="moved%d" % lo, tag=behind)
             gain_wide = gain_first if lo == 0 else gain_later
             places = mv_sb[:, lo // 16 : hi // 16]

@@ -225,8 +225,18 @@ def tile_picked_logcosh2_none_p_kernel(
             for lo, hi in ((0, HALF), (HALF, S)):
                 if c == CHUNKS - 1 - (lo == 0):
                     quantize(z_mx, lo, hi, z_bf16[:, PACK * lo : PACK * hi])
-                    for t in range(PACK):
+                    for t in (0, PACK - 1, 1, 2):
                         product(h_sums[t][:, lo:hi], w2_mx, t, z_mx[0][:, lo:hi], z_mx[1][:, lo:hi])
+
+        w3_mx = mx_tiles("w3")
+
+        def prepare_w3(copy, lo, hi, tag):
+            w3_bf16 = bf16_tile(hi - lo, "w3_bf16_%d" % lo, tag)
+            copy(
+                w3_bf16[:].rearrange("p (c i j) -> p c j i", i=PACK, j=PACK),
+                w3_raw[0][:, :, lo:hi].rearrange("p j (c i) -> p c j i", i=PACK),
+            )
+            quantize(w3_mx, lo, hi, w3_bf16[:])
 
         curved_part(0)
         z_mx = None
@@ -234,16 +244,12 @@ def tile_picked_logcosh2_none_p_kernel(
             if c + 1 < CHUNKS:
                 curved_part(c + 1)
             if c == CHUNKS - 2:
-                z_mx = mx_tiles("z", "curved3")
+                z_mx = mx_tiles("z", "curved2")
             finish_z(c, z_mx)
+            if c == 0:
+                prepare_w3(nc.vector.tensor_copy, HALF, N, "logs0")
 
-        w3_mx = mx_tiles("w3")
-        w3_bf16 = bf16_tile(N, "w3_bf16", "tails")
-        nc.scalar.copy(
-            w3_bf16[:].rearrange("p (c i j) -> p c j i", i=PACK, j=PACK),
-            w3_raw[0][:].rearrange("p j (c i) -> p c j i", i=PACK),
-        )
-        quantize(w3_mx, 0, N, w3_bf16[:])
+        prepare_w3(nc.scalar.copy, 0, HALF, "tails")
 
         last_sums = keep.tile([P, S], F32, name="last_sums")
         nc.vector.tensor_copy(last_sums[:], h_sums[PACK - 1][:])
@@ -255,7 +261,7 @@ def tile_picked_logcosh2_none_p_kernel(
 
         z2_mx = mx_tiles("z2")
         out_rows = out.rearrange("(t p) j -> p t j", p=P)
-        free_banks = list(z_banks)
+        logistic = keep.tile([P, S], F32, name="logistic")
         finished = []
         for lo, hi in LAST_CHUNKS:
             width = hi - lo
@@ -265,35 +271,43 @@ def tile_picked_logcosh2_none_p_kernel(
             places = mv_sb[:, lo // 16 : hi // 16]
             for t in range(PACK - 1):
                 nc.vector.tensor_tensor(moved[:, t, :], h[t][:].indirect(places), gain_wide[:, t, :], ALU.mult)
-            logistic = keep.tile([P, width], F32, name="logistic%d" % lo)
-            nc.scalar.activation(logistic[:], last_sums[:].indirect(places), ACT.Sigmoid, scale=2.0)
+            if lo % HALF == 0:
+                nc.scalar.activation(
+                    logistic[:, lo : lo + HALF],
+                    last_sums[:].indirect(mv_sb[:, lo // 16 : (lo + HALF) // 16]),
+                    ACT.Sigmoid,
+                    scale=2.0,
+                )
             nc.scalar.activation(
-                moved[:, PACK - 1, :], logistic[:], ACT.Identity, scale=last_gain[:, 0:1], bias=last_gain[:, 1:2]
+                moved[:, PACK - 1, :], logistic[:, lo:hi], ACT.Identity, scale=last_gain[:, 0:1], bias=last_gain[:, 1:2]
             )
-            z2_bf16 = bf16_tile(width, "z2_bf16_%d" % lo)
-            nc.scalar.copy(
-                z2_bf16[:].rearrange("p (c i t) -> p c t i", i=PACK, t=PACK),
-                moved[:, :, :].rearrange("p t (c i) -> p c t i", i=PACK),
-            )
-            quantize(z2_mx, lo, hi, z2_bf16[:])
-            per_bank = S // width
-            for t0 in range(0, PACK, per_bank):
-                sums = bank(free_banks.pop(0), "out_sums%d_%d" % (lo, t0))
-                for t in range(t0, t0 + per_bank):
-                    product(
-                        sums[:, (t - t0) * width : (t - t0 + 1) * width], w3_mx, t, z2_mx[0][:, lo:hi], z2_mx[1][:, lo:hi]
-                    )
-                finished.append((sums, lo, hi, t0))
+            for at in range(lo, hi, P):
+                z2_bf16 = bf16_tile(P, "z2_bf16_%d" % at)
+                nc.scalar.copy(
+                    z2_bf16[:].rearrange("p (c i t) -> p c t i", i=PACK, t=PACK),
+                    moved[:, :, at - lo : at - lo + P].rearrange("p t (c i) -> p c t i", i=PACK),
+                )
+                quantize(z2_mx, at, at + P, z2_bf16[:])
+                sums = bank(z_banks[at // P], "out_sums%d" % at)
+                for t in range(PACK):
+                    product(sums[:, t * P : (t + 1) * P], w3_mx, t, z2_mx[0][:, at : at + P], z2_mx[1][:, at : at + P])
+                finished.append((sums, at, at + P, 0))
 
         for sums, lo, hi, t0 in finished:
             width = hi - lo
             step = 2 if hi == S else S // width
             for t1 in range(t0, t0 + S // width, step):
-                result = keep.tile([P, step, width], F32, name="result%d_%d" % (lo, t1))
+                if lo == P:
+                    middle = keep.tile([P, 2, PACK, P], F32, align_bytes=64, name="middle", tag="z2_bf16_%d" % (S - P))
+                if lo in (P, 2 * P):
+                    result = middle[:, lo // P - 1]
+                else:
+                    result = keep.tile([P, step, width], F32, name="result%d_%d" % (lo, t1))
                 nc.vector.tensor_tensor(
-                    result[:],
+                    result[:, :, :],
                     sums[:, (t1 - t0) * width : (t1 - t0 + step) * width].rearrange("p (t j) -> p t j", j=width),
                     res_sb[:, t1 : t1 + step, lo:hi],
                     ALU.add,
                 )
-                nc.sync.dma_start(out_rows[:, t1 : t1 + step, lo:hi], result[:])
+                queue = nc.scalar if hi == S and t1 > 0 else nc.sync
+                queue.dma_start(out_rows[:, t1 : t1 + step, lo:hi], result[:, :, :])

from contextlib import ExitStack

import concourse.mybir as mybir
from concourse.masks import make_identity

K, T, S, H, N = 512, 2048, 512, 512, 512
FLOPS = 2 * S * (K * H + H * H + H * N)

F32 = mybir.dt.float32
BF16 = mybir.dt.bfloat16
I32 = mybir.dt.int32
U32 = mybir.dt.uint32
U16 = mybir.dt.uint16
U8 = mybir.dt.uint8
FP8X4 = mybir.dt.float8_e4m3fn_x4
ALU = mybir.AluOpType
ACT = mybir.ActivationFunctionType

P = 128
PACK = 4
CHUNKS = S // P
HALF = S // 2
LAST_CHUNKS = ((0, 256), (256, 384), (384, 512))


def tile_picked_logcosh2_none_p_kernel(
    tc, x_words, x_scales, w1, gn, w2, res, w3, offs, n1, n2, mv, out
):
    nc = tc.nc
    with ExitStack() as ctx:
        keep = ctx.enter_context(tc.tile_pool(name="keep", bufs=1))
        psum = ctx.enter_context(tc.psum_pool(name="psum", bufs=1))

        def bank(index, name):
            return psum.tile([P, S], F32, tag="bank%d" % index, name=name)

        def load_list(source, name):
            offsets = keep.tile([P, S // 16], U16, name=name)
            nc.sync.dma_start(offsets[:], source)
            return offsets

        def load_weight(weight, name, pieces):
            tiles = []
            for lo, hi in pieces:
                raw = keep.tile([P, PACK, hi - lo], F32, align_bytes=64, name="%s_raw%d" % (name, lo))
                nc.sync.dma_start(raw[:], weight.rearrange("(p j) c -> p j c", j=PACK)[:, :, lo:hi])
                tiles.append(raw)
            return tiles

        def bf16_tile(columns, name, tag=None):
            return keep.tile([P, columns * PACK], BF16, align_bytes=64, name=name, tag=tag or name)

        def mx_tiles(name, tag=None):
            codes = keep.tile([P, S], U32, align_bytes=64, name=name + "_codes", tag=tag or name + "_codes")
            scales = keep.tile([P, S], U8, align_bytes=64, name=name + "_scales")
            return codes, scales

        def quantize(operand, lo, hi, grouped):
            codes, scales = operand
            nc.vector.quantize_mx(out=codes[:, lo:hi].bitcast(FP8X4), scales=scales[:, lo:hi], in_=grouped)

        def product(target, weight, t, moving_codes, moving_scales):
            nc.tensor.matmul_mx(
                out=target,
                lhsT=weight[0][:, t * P : (t + 1) * P].bitcast(FP8X4),
                lhsT_scale=weight[1][:, t * P : (t + 1) * P],
                rhs=moving_codes.bitcast(FP8X4),
                rhs_scale=moving_scales,
                start=True,
                stop=True,
            )

        def deal_columns(copy, grouped, raw, m_lo, m_hi, first):
            dealt = grouped[:].rearrange("p (t m j) -> p m j t", t=PACK, j=PACK)
            source = raw[:].rearrange("p j (m t) -> p m j t", t=PACK)
            copy(dealt[:, m_lo:m_hi], source[:, m_lo - first : m_hi - first])

        def add_turned(target, source, start, stop):
            nc.tensor.matmul(target, source, identity[:], start=start, stop=stop, is_transpose=True)

        offs_sb = load_list(offs, "offs_sb")
        words = keep.tile([P, T], U32, name="words")
        nc.sync.dma_start(words[:].bitcast(I32), x_words[0].rearrange("p n t -> p (n t)").bitcast(I32))
        bytes_all = keep.tile([P, T], U8, name="bytes_all")
        nc.gpsimd.memset(bytes_all[:].bitcast(I32), 0)
        for q in range(4):
            nc.scalar.dma_start(
                bytes_all[32 * q : 32 * q + 4, :].bitcast(I32), x_scales[0][4 * q : 4 * q + 4, :].bitcast(I32)
            )
        w1_raw = load_weight(w1, "w1", ((0, HALF), (HALF, H)))
        gain = keep.tile([P, PACK], F32, name="gain")
        nc.sync.dma_start(gain[:], gn.rearrange("(p t) o -> p (t o)", t=PACK))
        n1_sb = load_list(n1, "n1_sb")
        n2_sb = load_list(n2, "n2_sb")
        w2_raw = load_weight(w2, "w2", ((0, H),))
        mv_sb = load_list(mv, "mv_sb")
        w3_raw = load_weight(w3, "w3", ((0, N),))
        res_sb = keep.tile([P, PACK, S], F32, name="res_sb")
        nc.sync.dma_start(res_sb[:], res.rearrange("(t p) j -> p t j", p=P))

        identity = keep.tile([P, P], F32, name="identity")
        make_identity(nc, identity[:])
        last_gain = keep.tile([P, 2], F32, name="last_gain")
        nc.gpsimd.tensor_scalar(last_gain[:, 0:1], gain[:, 3:4], 2.0, 0.0, ALU.mult, ALU.add)
        nc.gpsimd.tensor_scalar(last_gain[:, 1:2], gain[:, 3:4], -1.0, 0.0, ALU.mult, ALU.add)

        x_scale = keep.tile([P, S], U8, align_bytes=64, name="x_scale")
        x_codes = keep.tile([P, S], U32, align_bytes=64, name="x_codes")
        nc.vector.tensor_copy(x_scale[:], bytes_all[:].indirect(offs_sb[:]))

        nc.vector.tensor_copy(x_codes[:], words[:].indirect(offs_sb[:]))

        w1_mx = mx_tiles("w1")
        w1_bf16 = bf16_tile(H, "w1_bf16")
        deal_columns(nc.scalar.copy, w1_bf16, w1_raw[0], 0, 64, 0)
        deal_columns(nc.scalar.copy, w1_bf16, w1_raw[1], 64, 84, 64)
        deal_columns(nc.vector.tensor_copy, w1_bf16, w1_raw[1], 84, 128, 64)
        for t in range(PACK):
            quantize(w1_mx, t * P, (t + 1) * P, w1_bf16[:, t * S : (t + 1) * S])
        gain_first = keep.tile([P, PACK - 1, HALF], F32, align_bytes=64, name="gain_first", tag="w1_raw256")
        nc.scalar.copy(gain_first[:], gain[:, 0 : PACK - 1].unsqueeze(2).to_broadcast([P, PACK - 1, HALF]))
        gain_later = keep.tile([P, PACK - 1, P], F32, name="gain_later")
        nc.scalar.copy(gain_later[:], gain_first[:, :, :P])
        y = []
        for t in range(PACK):
            y_t = keep.tile([P, 2 * S], F32, align_bytes=64, name="y%d" % t)
            sums = bank(t, "y_sums%d" % t)
            if t == 0:
                second = bank(7, "y_sums0_second")
                product(sums[:, :HALF], w1_mx, t, x_codes[:, :HALF], x_scale[:, :HALF])
                product(second[:, :HALF], w1_mx, t, x_codes[:, HALF:], x_scale[:, HALF:])
                nc.scalar.copy(y_t[:, :HALF], sums[:, :HALF])
                nc.vector.tensor_copy(y_t[:, HALF:S], second[:, :HALF])
            else:
                product(sums[:], w1_mx, t, x_codes[:], x_scale[:])
                nc.scalar.copy(y_t[:, :S], sums[:])
            y.append(y_t)

        tails = keep.tile([P, CHUNKS, 2, PACK, P], F32, align_bytes=64, name="tails")
        all_sizes = []
        diff_banks = [4, 5, 6, 7, 0, 1, 2, 3, 4]
        waiting = []

        def squash():
            t, side, lo, hi = waiting.pop(0)
            nc.scalar.activation(
                tails[:, lo // P : hi // P, side, t, :],
                all_sizes[t][:, side, lo:hi].rearrange("p (c f) -> p c f", f=P),
                ACT.Tanh,
            )

        pieces = [(t, side, 0, S) for t in range(PACK) for side in range(2)][:-1]
        pieces.extend([(PACK - 1, 1, 0, HALF), (PACK - 1, 1, HALF, S)])
        all_others = []
        for t in range(PACK):
            all_sizes.append(keep.tile([P, 2, S], F32, align_bytes=64, name="sizes%d" % t))
            all_others.append(keep.tile([P, 2, S], F32, name="others%d" % t))

        def turn_own(index):
            t, side, lo, hi = pieces[index]
            diff = bank(diff_banks[index], "diff%d" % index)
            for at in range(0, hi - lo, P):
                add_turned(diff[:, at : at + P], y[t][:, lo + at : lo + at + P], at == 0, False)
            return diff

        next_diff = turn_own(0)
        for index, (t, side, lo, hi) in enumerate(pieces):
            diff = next_diff
            if index + 1 < len(pieces):
                next_diff = turn_own(index + 1)
            other = all_others[t][:, side, lo:hi]
            places = (n1_sb, n2_sb)[side][:, lo // 16 : hi // 16]
            nc.vector.tensor_scalar(other, y[t][:].indirect(places), -1.0, 0.0, ALU.mult, ALU.add)
            for at in range(0, hi - lo, P):
                add_turned(diff[:, at : at + P], other[:, at : at + P], False, at + P == hi - lo)
            nc.scalar.activation(all_sizes[t][:, side, lo:hi], diff[:, : hi - lo], ACT.Abs)
            if waiting:
                squash()
            waiting.append((t, side, lo, hi))
        squash()

        one = keep.tile([P, 1], F32, name="one")
        nc.scalar.activation(one[:], all_sizes[PACK - 1][:, 1, S - 1 : S], ACT.Identity, scale=0.0, bias=1.0)
        z_banks = (0, 1, 5, 6)
        h_banks = (2, 3, 4, 7)
        z_sums = [bank(z_banks[c], "z_sums%d" % c) for c in range(CHUNKS)]
        w2_mx = mx_tiles("w2")
        w2_bf16 = bf16_tile(H, "w2_bf16", "y3")
        deal_columns(nc.vector.tensor_copy, w2_bf16, w2_raw[0], 0, 128, 0)
        linear = keep.tile([P, PACK, S], F32, name="linear", tag="others3")
        for t in range(PACK):
            nc.vector.tensor_tensor(linear[:, t, :], all_sizes[t][:, 0, :], all_sizes[t][:, 1, :], ALU.subtract)
            for c in range(CHUNKS):
                add_turned(z_sums[c][:, t * P : (t + 1) * P], linear[:, t, c * P : (c + 1) * P], t == 0, False)
        quantize(w2_mx, 0, H, w2_bf16[:])

        h_sums = [bank(h_banks[t], "h_sums%d" % t) for t in range(PACK)]
        gain_by_place = gain[:].unsqueeze(1).to_broadcast([P, P, PACK])
        def curved_part(c):
            logs = keep.tile([P, 2, PACK, P], F32, align_bytes=64, name="logs%d" % c)
            curved = keep.tile([P, PACK, P], F32, align_bytes=64, name="curved%d" % c)
            for lo, hi in ((0, 2), (2, PACK)) if c == CHUNKS - 1 else ((0, PACK),):
                nc.scalar.activation(logs[:, :, lo:hi, :], tails[:, c, :, lo:hi, :], ACT.Ln, bias=one[:])
                if c == CHUNKS - 1:
                    nc.vector.tensor_tensor(curved[:, lo:hi], logs[:, 1, lo:hi], logs[:, 0, lo:hi], ALU.subtract)
                else:
                    nc.vector.tensor_scalar(curved[:, lo:hi], logs[:, 0, lo:hi], -1.0, None, ALU.mult)
                    for t in range(lo, hi):
                        add_turned(z_sums[c][:, t * P : (t + 1) * P], logs[:, 1, t, :], False, False)
                for t in range(lo, hi):
                    add_turned(z_sums[c][:, t * P : (t + 1) * P], curved[:, t, :], False, t == PACK - 1)
            if c == CHUNKS - 1:
                warm = keep.tile([P, 1], F32, name="warm")
                nc.scalar.activation(warm[:], logs[:, 0, PACK - 1, 0:1], ACT.Sigmoid)

        z_bf16 = bf16_tile(S, "z_bf16")

        def finish_z(c, z_mx):
            nc.vector.tensor_tensor(
                z_bf16[:, c * S : (c + 1) * S].rearrange("p (j t) -> p j t", t=PACK),
                z_sums[c][:].rearrange("p (t j) -> p j t", t=PACK),
                gain_by_place,
                ALU.mult,
            )
            for lo, hi in ((0, HALF), (HALF, S)):
                if c == CHUNKS - 1 - (lo == 0):
                    quantize(z_mx, lo, hi, z_bf16[:, PACK * lo : PACK * hi])
                    for t in (0, PACK - 1, 1, 2):
                        product(h_sums[t][:, lo:hi], w2_mx, t, z_mx[0][:, lo:hi], z_mx[1][:, lo:hi])

        w3_mx = mx_tiles("w3")

        def prepare_w3(copy, lo, hi, tag):
            w3_bf16 = bf16_tile(hi - lo, "w3_bf16_%d" % lo, tag)
            copy(
                w3_bf16[:].rearrange("p (c i j) -> p c j i", i=PACK, j=PACK),
                w3_raw[0][:, :, lo:hi].rearrange("p j (c i) -> p c j i", i=PACK),
            )
            quantize(w3_mx, lo, hi, w3_bf16[:])

        curved_part(0)
        z_mx = None
        for c in range(CHUNKS):
            if c + 1 < CHUNKS:
                curved_part(c + 1)
            if c == CHUNKS - 2:
                z_mx = mx_tiles("z", "curved2")
            finish_z(c, z_mx)
            if c == 0:
                prepare_w3(nc.vector.tensor_copy, HALF, N, "logs0")

        prepare_w3(nc.scalar.copy, 0, HALF, "tails")

        last_sums = keep.tile([P, S], F32, name="last_sums")
        nc.vector.tensor_copy(last_sums[:], h_sums[PACK - 1][:])
        h = []
        for t in range(PACK - 1):
            h_t = keep.tile([P, S], F32, name="h%d" % t)
            nc.scalar.activation(h_t[:], h_sums[t][:], ACT.Tanh)
            h.append(h_t)

        z2_mx = mx_tiles("z2")
        out_rows = out.rearrange("(t p) j -> p t j", p=P)
        logistic = keep.tile([P, S], F32, name="logistic")
        finished = []
        for lo, hi in LAST_CHUNKS:
            width = hi - lo
            behind = {0: "moved0", HALF: "w1_raw256", S - P: "z2_bf16_0"}[lo]
            moved = keep.tile([P, PACK, width], F32, align_bytes=64, name="moved%d" % lo, tag=behind)
            gain_wide = gain_first if lo == 0 else gain_later
            places = mv_sb[:, lo // 16 : hi // 16]
            for t in range(PACK - 1):
                nc.vector.tensor_tensor(moved[:, t, :], h[t][:].indirect(places), gain_wide[:, t, :], ALU.mult)
            if lo % HALF == 0:
                nc.scalar.activation(
                    logistic[:, lo : lo + HALF],
                    last_sums[:].indirect(mv_sb[:, lo // 16 : (lo + HALF) // 16]),
                    ACT.Sigmoid,
                    scale=2.0,
                )
            nc.scalar.activation(
                moved[:, PACK - 1, :], logistic[:, lo:hi], ACT.Identity, scale=last_gain[:, 0:1], bias=last_gain[:, 1:2]
            )
            for at in range(lo, hi, P):
                z2_bf16 = bf16_tile(P, "z2_bf16_%d" % at)
                nc.scalar.copy(
                    z2_bf16[:].rearrange("p (c i t) -> p c t i", i=PACK, t=PACK),
                    moved[:, :, at - lo : at - lo + P].rearrange("p t (c i) -> p c t i", i=PACK),
                )
                quantize(z2_mx, at, at + P, z2_bf16[:])
                sums = bank(z_banks[at // P], "out_sums%d" % at)
                for t in range(PACK):
                    product(sums[:, t * P : (t + 1) * P], w3_mx, t, z2_mx[0][:, at : at + P], z2_mx[1][:, at : at + P])
                finished.append((sums, at, at + P, 0))

        for sums, lo, hi, t0 in finished:
            width = hi - lo
            step = 2 if hi == S else S // width
            for t1 in range(t0, t0 + S // width, step):
                if lo == P:
                    middle = keep.tile([P, 2, PACK, P], F32, align_bytes=64, name="middle", tag="z2_bf16_%d" % (S - P))
                if lo in (P, 2 * P):
                    result = middle[:, lo // P - 1]
                else:
                    result = keep.tile([P, step, width], F32, name="result%d_%d" % (lo, t1))
                nc.vector.tensor_tensor(
                    result[:, :, :],
                    sums[:, (t1 - t0) * width : (t1 - t0 + step) * width].rearrange("p (t j) -> p t j", j=width),
                    res_sb[:, t1 : t1 + step, lo:hi],
                    ALU.add,
                )
                queue = nc.scalar if hi == S and t1 > 0 else nc.sync
                queue.dma_start(out_rows[:, t1 : t1 + step, lo:hi], result[:, :, :])
